import numpy as np
import ml_dtypes


def mxq(x, axis, fmt="e4m3"):
    dtype, down = {"e4m3": (ml_dtypes.float8_e4m3fn, 7), "e5m2": (ml_dtypes.float8_e5m2, 14)}[fmt]
    v = np.moveaxis(np.asarray(x, np.float32).astype(ml_dtypes.bfloat16).astype(np.float64), axis, -1)
    blocks = v.reshape(v.shape[:-1] + (-1, 32))
    amax = np.abs(blocks).max(-1, keepdims=True)
    byte = np.maximum(np.where(amax > 0, np.frexp(amax)[1] - 1 + 127, 0) - down, 1)
    scale = np.exp2(byte - 127.0)
    codes = (blocks / scale).astype(np.float32).astype(dtype).astype(np.float64)
    return np.moveaxis((codes * scale).reshape(v.shape), -1, axis)


WIDE = False


def mx_kscale(k):
    if not WIDE:
        return np.ones(k)
    levels = np.array([10, -10, 5, -5, 0])
    if k % 512:
        return np.exp2(np.random.permutation(np.resize(levels, k // 32))).repeat(32)
    a = np.empty((k // 512, 16))
    for p in range(k // 512):
        a[p, :8] = np.random.permutation(np.resize(levels, 8))
        for g in range(8):
            far = levels[np.abs(levels - a[p, g]) >= 10]
            a[p, g + 8] = far[np.random.randint(len(far))]
    return np.exp2(a.ravel()).repeat(32)


def f64(x):
    return np.asarray(x).astype(np.float64)


def striped(idx):
    return np.tile(idx.reshape(-1, 16).T, (8, 1)).astype(np.uint16)


def unstriped(offs):
    return offs[:16].T.reshape(-1).astype(np.int64)


def relu(v):
    return np.maximum(v, 0.0)


K, T, S, N = 512, 2048, 1024, 256


def setup_inputs():
    n = np.random.standard_normal
    s = mx_kscale(K)[:, None]
    return {
        "xT": (n((K, T)) * s).astype(np.float32),
        "w1": (n((K, N)) / np.sqrt(3 * K) / s).astype(np.float32),
        "w2": (n((K, N)) / np.sqrt(3 * K) / s).astype(np.float32),
        "w3": (n((K, N)) / np.sqrt(3 * K) / s).astype(np.float32),
        "offs": striped(np.random.permutation(T)[:S]),
    }


def reference(xT, w1, w2, w3, offs):
    xq = mxq(f64(xT)[:, unstriped(offs)], 0, "e4m3")
    y0 = mxq(f64(w1), 0, "e4m3").T @ xq
    y1 = mxq(f64(w2), 0, "e4m3").T @ xq
    y2 = mxq(f64(w3), 0, "e4m3").T @ xq
    return relu(y0 + np.pad(y1, ((0, 0), (1, 0)))[:, :S] + np.pad(y2, ((0, 0), (2, 0)))[:, :S])

@@ -1,0 +1,182 @@
+from contextlib import ExitStack
+
+import concourse.mybir as mybir
+
+K, T, S, N = 512, 2048, 1024, 256
+TAPS = 3
+FLOPS = 2 * TAPS * K * N * S
+
+F32 = mybir.dt.float32
+BF16 = mybir.dt.bfloat16
+I32 = mybir.dt.int32
+U32 = mybir.dt.uint32
+U16 = mybir.dt.uint16
+U8 = mybir.dt.uint8
+FP8X4 = mybir.dt.float8_e4m3fn_x4
+COPY = mybir.ActivationFunctionType.Copy
+RELU = mybir.ActivationFunctionType.Relu
+
+P = 128
+COLS = 64
+BLOCK_ROWS = (8, 4, 4)
+BLOCK_START = (0, 512, 768)
+HALF = S // 2
+NB = len(BLOCK_ROWS)
+HALO = TAPS - 1
+LEAD = 32
+GW = 576
+
+
+def tile_picked_listconv_relu_e_kernel(tc, xT, w1, w2, w3, offs, out):
+    nc = tc.nc
+    with ExitStack() as ctx:
+        keep = ctx.enter_context(tc.tile_pool(name="keep", bufs=1))
+        psum = ctx.enter_context(tc.psum_pool(name="psum", bufs=1))
+
+        x_rows = xT.rearrange("(p j) t -> p j t", j=4)
+        offsets = keep.tile([P, S // 16], U16, name="offsets")
+
+        def load_x(u, t0, t1):
+            raw = keep.tile([P, 2, t1 - t0], F32, name=f"x_raw_{u}_{t0}")
+            nc.sync.dma_start(out=raw[:], in_=x_rows[:, 2 * u : 2 * u + 2, t0:t1])
+            return raw
+
+        a_cuts = [(0, 512), (512, 1024), (1024, 2048)]
+        b_cuts = [(0, 512), (512, 1024), (1024, 1536), (1536, 2048)]
+        raw_a = [load_x(0, *a_cuts[0])]
+        nc.sync.dma_start(offsets[:], offs)
+        raw_a.extend(load_x(0, *c) for c in a_cuts[1:])
+        raw_b = [load_x(1, *c) for c in b_cuts]
+        w_raw = []
+        for d, w in enumerate((w1, w2, w3)):
+            raw = keep.tile([P, 4, N], F32, name=f"w_raw_{d}")
+            nc.sync.dma_start(out=raw[:], in_=w.rearrange("(p j) n -> p j n", j=4))
+            w_raw.append(raw)
+
+        pairs = [keep.tile([P, T], U32, name=f"pairs_{u}") for u in range(2)]
+
+        def pair_views(u, raw, t_raw, t0, t1):
+            dst = pairs[u][:, t0:t1].bitcast(BF16).rearrange("p (t e) -> p t e", e=2)
+            src = raw[:, :, t0 - t_raw : t1 - t_raw].rearrange("p e t -> p t e")
+            return dst, src
+
+        picked = keep.tile([P, 3, GW], I32, name="picked")
+        nc.vector.memset(picked[:, 0:3:2, LEAD : LEAD + HALO], 0)
+
+        def gather(u, h):
+            first = max(h * HALF - LEAD, 0)
+            last = (h + 1) * HALF
+            at = first - (h * HALF - LEAD) + HALO
+            nc.vector.tensor_copy(
+                picked[:, h if u == 0 else 2, at : at + last - first].bitcast(U32),
+                pairs[u][:].indirect(offsets[:, first // 16 : last // 16]),
+            )
+
+        for raw, (t0, t1) in zip(raw_a, a_cuts):
+            nc.vector.tensor_copy(*pair_views(0, raw, t0, t0, t1))
+        for h in range(2):
+            gather(0, h)
+        for raw, (t0, t1) in zip(raw_b[:-1], b_cuts[:-1]):
+            dst, src = pair_views(1, raw, t0, t0, t1)
+            nc.scalar.activation(dst, src, COPY)
+        t0, t1 = b_cuts[-1]
+        split = t0 + 160
+        dst, src = pair_views(1, raw_b[-1], t0, t0, split)
+        nc.scalar.activation(dst, src, COPY)
+        nc.vector.tensor_copy(*pair_views(1, raw_b[-1], t0, split, t1))
+
+        woven = [keep.tile([P, (r + HALO) * COLS * 2], I32, name=f"woven_{b}", align_bytes=64) for b, r in enumerate(BLOCK_ROWS)]
+        x_codes = [keep.tile([P, (r + HALO) * COLS], U32, name=f"x_codes_{b}", align_bytes=64) for b, r in enumerate(BLOCK_ROWS)]
+        x_scales = [keep.tile([P, (r + HALO) * COLS], U8, name=f"x_scales_{b}", align_bytes=64) for b, r in enumerate(BLOCK_ROWS)]
+
+        def weave_views(b, r0, r1, dtype):
+            rows = BLOCK_ROWS[b]
+            h = BLOCK_START[b] // HALF
+            base = LEAD + BLOCK_START[b] % HALF + (r0 // rows) * rows
+            src = picked[:, h : 3 : 2 - h, base : base + rows * COLS].bitcast(dtype)
+            src = src.rearrange("p u (cc c2 r) -> p cc r c2 u", c2=2, r=rows)[:, :, r0 % rows : r0 % rows + r1 - r0]
+            dst = woven[b][:, r0 * COLS * 2 : r1 * COLS * 2].bitcast(dtype)
+            dst = dst.rearrange("p (r cc c2 u) -> p cc r c2 u", c2=2, u=2, r=r1 - r0)
+            return dst, src
+
+        def weave_vector(b, r0, r1):
+            nc.vector.tensor_copy(*weave_views(b, r0, r1, I32))
+
+        def weave_scalar(b, r0, r1):
+            nc.scalar.copy(*weave_views(b, r0, r1, U32))
+
+        def quantize_x(b, r0, r1):
+            nc.vector.quantize_mx(
+                out=x_codes[b][:, r0 * COLS : r1 * COLS].bitcast(FP8X4),
+                scales=x_scales[b][:, r0 * COLS : r1 * COLS],
+                in_=woven[b][:, r0 * COLS * 2 : r1 * COLS * 2].bitcast(BF16),
+            )
+
+        w_bf = [keep.tile([P, N * 4], BF16, name=f"w_bf_{d}", align_bytes=64) for d in range(TAPS)]
+        w_codes = [keep.tile([P, N], U32, name=f"w_codes_{d}", align_bytes=64) for d in range(TAPS)]
+        w_scales = [keep.tile([P, N], U8, name=f"w_scales_{d}", align_bytes=64) for d in range(TAPS)]
+
+        def cast_w(d):
+            nc.scalar.activation(
+                w_bf[d][:].rearrange("p (c i j) -> p c j i", i=4, j=4),
+                w_raw[d][:].rearrange("p j (c i) -> p c j i", i=4),
+                COPY,
+            )
+
+        def quantize_w(d):
+            nc.vector.quantize_mx(out=w_codes[d][:].bitcast(FP8X4), scales=w_scales[d][:], in_=w_bf[d][:])
+
+        acc = [[psum.tile([P, r * COLS], F32, name=f"acc_{b}_{m}") for m in range(2)] for b, r in enumerate(BLOCK_ROWS)]
+
+        def product(b, m, d):
+            cols = slice((HALO - d) * COLS, (HALO - d + BLOCK_ROWS[b]) * COLS)
+            nc.tensor.matmul_mx(
+                out=acc[b][m][:],
+                lhsT=w_codes[d][:, m * P : (m + 1) * P].bitcast(FP8X4),
+                lhsT_scale=w_scales[d][:, m * P : (m + 1) * P],
+                rhs=x_codes[b][:, cols].bitcast(FP8X4),
+                rhs_scale=x_scales[b][:, cols],
+                start=(d == 0),
+                stop=(d == TAPS - 1),
+            )
+
+        def finish(b, m, on_vector):
+            rows = BLOCK_ROWS[b]
+            res = keep.tile([P, rows * COLS], F32, name=f"res_{b}_{m}")
+            dst = res[:].rearrange("p (c r) -> p c r", r=rows)
+            src = acc[b][m][:].rearrange("p (r c) -> p c r", r=rows)
+            if on_vector:
+                nc.vector.tensor_scalar_max(dst, src, 0.0)
+            else:
+                nc.scalar.activation(dst, src, RELU)
+            nc.sync.dma_start(out=out[m * P : (m + 1) * P, BLOCK_START[b] : BLOCK_START[b] + rows * COLS], in_=res[:])
+
+        cast_w(0)
+        gather(1, 0)
+        weave_vector(0, 0, 8)
+        weave_scalar(0, 8, 10)
+        cast_w(1)
+        cast_w(2)
+        quantize_w(0)
+        quantize_x(0, 0, 8)
+        quantize_x(0, 8, 10)
+        quantize_w(1)
+        gather(1, 1)
+        quantize_w(2)
+        for m, d in ((0, 0), (0, 1), (1, 0), (0, 2), (1, 1), (1, 2)):
+            product(0, m, d)
+        weave_vector(1, 0, 4)
+        weave_scalar(1, 4, 6)
+        weave_scalar(2, 0, 4)
+        weave_scalar(2, 4, 6)
+        quantize_x(1, 0, 4)
+        quantize_x(1, 4, 6)
+        quantize_x(2, 0, 4)
+        quantize_x(2, 4, 6)
+        finish(0, 0, False)
+        finish(0, 1, True)
+        for b in range(1, NB):
+            for m in range(2):
+                for d in range(TAPS):
+                    product(b, m, d)
+                finish(b, m, m == 1)

@@ -20,11 +20,12 @@ P = 128
 COLS = 64
 BLOCK_ROWS = (8, 4, 4)
 BLOCK_START = (0, 512, 768)
-HALF = S // 2
 NB = len(BLOCK_ROWS)
+HALF = S // 2
 HALO = TAPS - 1
 LEAD = 32
 GW = 576
+ROW_WORDS = 2 * COLS
 
 
 def tile_picked_listconv_relu_e_kernel(tc, xT, w1, w2, w3, offs, out):
@@ -41,17 +42,16 @@ def tile_picked_listconv_relu_e_kernel(tc, xT, w1, w2, w3, offs, out):
             nc.sync.dma_start(out=raw[:], in_=x_rows[:, 2 * u : 2 * u + 2, t0:t1])
             return raw
 
-        a_cuts = [(0, 512), (512, 1024), (1024, 2048)]
-        b_cuts = [(0, 512), (512, 1024), (1024, 1536), (1536, 2048)]
-        raw_a = [load_x(0, *a_cuts[0])]
+        raw_a0 = load_x(0, 0, 1024)
+        raw_a1 = load_x(0, 1024, 2048)
         nc.sync.dma_start(offsets[:], offs)
-        raw_a.extend(load_x(0, *c) for c in a_cuts[1:])
-        raw_b = [load_x(1, *c) for c in b_cuts]
-        w_raw = []
-        for d, w in enumerate((w1, w2, w3)):
-            raw = keep.tile([P, 4, N], F32, name=f"w_raw_{d}")
-            nc.sync.dma_start(out=raw[:], in_=w.rearrange("(p j) n -> p j n", j=4))
-            w_raw.append(raw)
+        raw_b0 = load_x(1, 0, 1024)
+        raw_b1 = load_x(1, 1024, 1536)
+        raw_b2 = load_x(1, 1536, 2048)
+        w_raw = {}
+        for d in (2, 1, 0):
+            w_raw[d] = keep.tile([P, 4, N], F32, name=f"w_raw_{d}", tag=f"w_raw_{d}", align_bytes=64)
+            nc.sync.dma_start(out=w_raw[d][:], in_=(w1, w2, w3)[d].rearrange("(p j) n -> p j n", j=4))
 
         pairs = [keep.tile([P, T], U32, name=f"pairs_{u}") for u in range(2)]
 
@@ -60,43 +60,56 @@ def tile_picked_listconv_relu_e_kernel(tc, xT, w1, w2, w3, offs, out):
             src = raw[:, :, t0 - t_raw : t1 - t_raw].rearrange("p e t -> p t e")
             return dst, src
 
-        picked = keep.tile([P, 3, GW], I32, name="picked")
-        nc.vector.memset(picked[:, 0:3:2, LEAD : LEAD + HALO], 0)
+        def pair_vector(u, raw, t_raw, t0, t1):
+            nc.vector.tensor_copy(*pair_views(u, raw, t_raw, t0, t1))
+
+        def pair_scalar(u, raw, t_raw, t0, t1):
+            dst, src = pair_views(u, raw, t_raw, t0, t1)
+            nc.scalar.activation(dst, src, COPY)
+
+        picked = [keep.tile([P, 2 * GW], I32, name=f"picked_{h}", align_bytes=64) for h in range(2)]
+        both = [t[:].rearrange("p (u g) -> p u g", u=2) for t in picked]
+        nc.vector.memset(both[0][:, :, LEAD : LEAD + HALO], 0)
 
         def gather(u, h):
             first = max(h * HALF - LEAD, 0)
             last = (h + 1) * HALF
             at = first - (h * HALF - LEAD) + HALO
             nc.vector.tensor_copy(
-                picked[:, h if u == 0 else 2, at : at + last - first].bitcast(U32),
+                both[h][:, u, at : at + last - first].bitcast(U32),
                 pairs[u][:].indirect(offsets[:, first // 16 : last // 16]),
             )
 
-        for raw, (t0, t1) in zip(raw_a, a_cuts):
-            nc.vector.tensor_copy(*pair_views(0, raw, t0, t0, t1))
+        pair_vector(0, raw_a0, 0, 0, 1024)
+        pair_scalar(0, raw_a1, 1024, 1024, 1344)
+        pair_vector(0, raw_a1, 1024, 1344, 2048)
         for h in range(2):
             gather(0, h)
-        for raw, (t0, t1) in zip(raw_b[:-1], b_cuts[:-1]):
-            dst, src = pair_views(1, raw, t0, t0, t1)
-            nc.scalar.activation(dst, src, COPY)
-        t0, t1 = b_cuts[-1]
-        split = t0 + 160
-        dst, src = pair_views(1, raw_b[-1], t0, t0, split)
-        nc.scalar.activation(dst, src, COPY)
-        nc.vector.tensor_copy(*pair_views(1, raw_b[-1], t0, split, t1))
+        pair_scalar(1, raw_b0, 0, 0, 1024)
+        pair_vector(1, raw_b1, 1024, 1024, 1536)
+        pair_scalar(1, raw_b2, 1536, 1536, 1664)
+        pair_vector(1, raw_b2, 1536, 1664, 2048)
 
-        woven = [keep.tile([P, (r + HALO) * COLS * 2], I32, name=f"woven_{b}", align_bytes=64) for b, r in enumerate(BLOCK_ROWS)]
-        x_codes = [keep.tile([P, (r + HALO) * COLS], U32, name=f"x_codes_{b}", align_bytes=64) for b, r in enumerate(BLOCK_ROWS)]
+        w_bf_2 = keep.tile([P, N * 4], BF16, name="w_bf_2", tag="w_bf_2", align_bytes=64)
+        w_bf_0 = keep.tile([P, N * 4], BF16, name="w_bf_0", align_bytes=64)
+        w_bf = [w_bf_0[:], picked[1][:, GW : GW + 2 * N].bitcast(BF16), w_bf_2[:]]
+        woven_0 = keep.tile([P, 8 * ROW_WORDS], I32, name="woven_0", align_bytes=64)
+        halo_0 = keep.tile([P, HALO * ROW_WORDS], I32, name="halo_0", tag="w_raw_2", align_bytes=64)
+        woven_12 = keep.tile([P, 12 * ROW_WORDS], I32, name="woven_12", tag="w_raw_0", align_bytes=64)
+        x_codes = [keep.tile([P, (r + HALO) * COLS], U32, name=f"x_codes_{b}", tag=("w_bf_2", "x_codes_1", "x_codes_2")[b], align_bytes=64) for b, r in enumerate(BLOCK_ROWS)]
         x_scales = [keep.tile([P, (r + HALO) * COLS], U8, name=f"x_scales_{b}", align_bytes=64) for b, r in enumerate(BLOCK_ROWS)]
+
+        def woven_rows(b, r0, r1):
+            if b == 0:
+                return halo_0[:] if r0 == 8 else woven_0[:, r0 * ROW_WORDS : r1 * ROW_WORDS]
+            return woven_12[:, (6 * (b - 1) + r0) * ROW_WORDS : (6 * (b - 1) + r1) * ROW_WORDS]
 
         def weave_views(b, r0, r1, dtype):
             rows = BLOCK_ROWS[b]
-            h = BLOCK_START[b] // HALF
             base = LEAD + BLOCK_START[b] % HALF + (r0 // rows) * rows
-            src = picked[:, h : 3 : 2 - h, base : base + rows * COLS].bitcast(dtype)
+            src = both[BLOCK_START[b] // HALF][:, :, base : base + rows * COLS].bitcast(dtype)
             src = src.rearrange("p u (cc c2 r) -> p cc r c2 u", c2=2, r=rows)[:, :, r0 % rows : r0 % rows + r1 - r0]
-            dst = woven[b][:, r0 * COLS * 2 : r1 * COLS * 2].bitcast(dtype)
-            dst = dst.rearrange("p (r cc c2 u) -> p cc r c2 u", c2=2, u=2, r=r1 - r0)
+            dst = woven_rows(b, r0, r1).bitcast(dtype).rearrange("p (r cc c2 u) -> p cc r c2 u", c2=2, u=2, r=r1 - r0)
             return dst, src
 
         def weave_vector(b, r0, r1):
@@ -109,22 +122,21 @@ def tile_picked_listconv_relu_e_kernel(tc, xT, w1, w2, w3, offs, out):
             nc.vector.quantize_mx(
                 out=x_codes[b][:, r0 * COLS : r1 * COLS].bitcast(FP8X4),
                 scales=x_scales[b][:, r0 * COLS : r1 * COLS],
-                in_=woven[b][:, r0 * COLS * 2 : r1 * COLS * 2].bitcast(BF16),
+                in_=woven_rows(b, r0, r1).bitcast(BF16),
             )
 
-        w_bf = [keep.tile([P, N * 4], BF16, name=f"w_bf_{d}", align_bytes=64) for d in range(TAPS)]
         w_codes = [keep.tile([P, N], U32, name=f"w_codes_{d}", align_bytes=64) for d in range(TAPS)]
         w_scales = [keep.tile([P, N], U8, name=f"w_scales_{d}", align_bytes=64) for d in range(TAPS)]
 
         def cast_w(d):
             nc.scalar.activation(
-                w_bf[d][:].rearrange("p (c i j) -> p c j i", i=4, j=4),
+                w_bf[d].rearrange("p (c i j) -> p c j i", i=4, j=4),
                 w_raw[d][:].rearrange("p j (c i) -> p c j i", i=4),
                 COPY,
             )
 
         def quantize_w(d):
-            nc.vector.quantize_mx(out=w_codes[d][:].bitcast(FP8X4), scales=w_scales[d][:], in_=w_bf[d][:])
+            nc.vector.quantize_mx(out=w_codes[d][:].bitcast(FP8X4), scales=w_scales[d][:], in_=w_bf[d])
 
         acc = [[psum.tile([P, r * COLS], F32, name=f"acc_{b}_{m}") for m in range(2)] for b, r in enumerate(BLOCK_ROWS)]
 
@@ -136,47 +148,50 @@ def tile_picked_listconv_relu_e_kernel(tc, xT, w1, w2, w3, offs, out):
                 lhsT_scale=w_scales[d][:, m * P : (m + 1) * P],
                 rhs=x_codes[b][:, cols].bitcast(FP8X4),
                 rhs_scale=x_scales[b][:, cols],
-                start=(d == 0),
-                stop=(d == TAPS - 1),
+                start=(d == TAPS - 1),
+                stop=(d == 0),
             )
 
         def finish(b, m, on_vector):
             rows = BLOCK_ROWS[b]
-            res = keep.tile([P, rows * COLS], F32, name=f"res_{b}_{m}")
-            dst = res[:].rearrange("p (c r) -> p c r", r=rows)
+            if (b, m) == (1, 0):
+                res = woven_rows(2, 4, 6).bitcast(F32)
+            else:
+                res = keep.tile([P, rows * COLS], F32, name=f"res_{b}_{m}")[:]
+            dst = res.rearrange("p (c r) -> p c r", r=rows)
             src = acc[b][m][:].rearrange("p (r c) -> p c r", r=rows)
             if on_vector:
                 nc.vector.tensor_scalar_max(dst, src, 0.0)
             else:
                 nc.scalar.activation(dst, src, RELU)
-            nc.sync.dma_start(out=out[m * P : (m + 1) * P, BLOCK_START[b] : BLOCK_START[b] + rows * COLS], in_=res[:])
+            nc.sync.dma_start(out=out[m * P : (m + 1) * P, BLOCK_START[b] : BLOCK_START[b] + rows * COLS], in_=res)
 
-        cast_w(0)
+        cast_w(2)
         gather(1, 0)
         weave_vector(0, 0, 8)
         weave_scalar(0, 8, 10)
         cast_w(1)
-        cast_w(2)
-        quantize_w(0)
-        quantize_x(0, 0, 8)
-        quantize_x(0, 8, 10)
-        quantize_w(1)
-        gather(1, 1)
+        cast_w(0)
         quantize_w(2)
-        for m, d in ((0, 0), (0, 1), (1, 0), (0, 2), (1, 1), (1, 2)):
-            product(0, m, d)
+        quantize_x(0, 0, 8)
+        quantize_w(1)
+        quantize_x(0, 8, 10)
+        gather(1, 1)
+        quantize_w(0)
+        for d in (2, 1, 0):
+            for m in range(2):
+                product(0, m, d)
         weave_vector(1, 0, 4)
         weave_scalar(1, 4, 6)
-        weave_scalar(2, 0, 4)
+        weave_vector(2, 0, 4)
         weave_scalar(2, 4, 6)
-        quantize_x(1, 0, 4)
-        quantize_x(1, 4, 6)
-        quantize_x(2, 0, 4)
-        quantize_x(2, 4, 6)
+        for b in range(1, NB):
+            quantize_x(b, 0, 4)
+            quantize_x(b, 4, 6)
         finish(0, 0, False)
-        finish(0, 1, True)
+        finish(0, 1, False)
         for b in range(1, NB):
             for m in range(2):
-                for d in range(TAPS):
+                for d in (2, 1, 0):
                     product(b, m, d)
-                finish(b, m, m == 1)
+                finish(b, m, m == 0)

@@ -32,6 +32,7 @@ def tile_picked_listconv_relu_e_kernel(tc, xT, w1, w2, w3, offs, out):
     nc = tc.nc
     with ExitStack() as ctx:
         keep = ctx.enter_context(tc.tile_pool(name="keep", bufs=1))
+        shared = ctx.enter_context(tc.tile_pool(name="shared", bufs=1))
         psum = ctx.enter_context(tc.psum_pool(name="psum", bufs=1))
 
         x_rows = xT.rearrange("(p j) t -> p j t", j=4)
@@ -50,7 +51,10 @@ def tile_picked_listconv_relu_e_kernel(tc, xT, w1, w2, w3, offs, out):
         raw_b2 = load_x(1, 1536, 2048)
         w_raw = {}
         for d in (2, 1, 0):
-            w_raw[d] = keep.tile([P, 4, N], F32, name=f"w_raw_{d}", tag=f"w_raw_{d}", align_bytes=64)
+            if d == 2:
+                w_raw[d] = shared.tile([P, 4, N], F32, name="w_raw_2", align_bytes=64, offset=0)
+            else:
+                w_raw[d] = keep.tile([P, 4, N], F32, name=f"w_raw_{d}", tag=f"w_raw_{d}", align_bytes=64)
             nc.sync.dma_start(out=w_raw[d][:], in_=(w1, w2, w3)[d].rearrange("(p j) n -> p j n", j=4))
 
         pairs = [keep.tile([P, T], U32, name=f"pairs_{u}") for u in range(2)]
@@ -90,13 +94,14 @@ def tile_picked_listconv_relu_e_kernel(tc, xT, w1, w2, w3, offs, out):
         pair_scalar(1, raw_b2, 1536, 1536, 1664)
         pair_vector(1, raw_b2, 1536, 1664, 2048)
 
-        w_bf_2 = keep.tile([P, N * 4], BF16, name="w_bf_2", tag="w_bf_2", align_bytes=64)
+        w_bf_2 = keep.tile([P, N * 4], BF16, name="w_bf_2", align_bytes=64)
         w_bf_0 = keep.tile([P, N * 4], BF16, name="w_bf_0", align_bytes=64)
         w_bf = [w_bf_0[:], picked[1][:, GW : GW + 2 * N].bitcast(BF16), w_bf_2[:]]
         woven_0 = keep.tile([P, 8 * ROW_WORDS], I32, name="woven_0", align_bytes=64)
-        halo_0 = keep.tile([P, HALO * ROW_WORDS], I32, name="halo_0", tag="w_raw_2", align_bytes=64)
+        halo_0 = shared.tile([P, HALO * ROW_WORDS], I32, name="halo_0", align_bytes=64, offset=0)
         woven_12 = keep.tile([P, 12 * ROW_WORDS], I32, name="woven_12", tag="w_raw_0", align_bytes=64)
-        x_codes = [keep.tile([P, (r + HALO) * COLS], U32, name=f"x_codes_{b}", tag=("w_bf_2", "x_codes_1", "x_codes_2")[b], align_bytes=64) for b, r in enumerate(BLOCK_ROWS)]
+        x_codes = [shared.tile([P, 10 * COLS], U32, name="x_codes_0", align_bytes=64, offset=1024)]
+        x_codes.extend(keep.tile([P, 6 * COLS], U32, name=f"x_codes_{b}", align_bytes=64) for b in range(1, NB))
         x_scales = [keep.tile([P, (r + HALO) * COLS], U8, name=f"x_scales_{b}", align_bytes=64) for b, r in enumerate(BLOCK_ROWS)]
 
         def woven_rows(b, r0, r1):
@@ -108,8 +113,10 @@ def tile_picked_listconv_relu_e_kernel(tc, xT, w1, w2, w3, offs, out):
             rows = BLOCK_ROWS[b]
             base = LEAD + BLOCK_START[b] % HALF + (r0 // rows) * rows
             src = both[BLOCK_START[b] // HALF][:, :, base : base + rows * COLS].bitcast(dtype)
-            src = src.rearrange("p u (cc c2 r) -> p cc r c2 u", c2=2, r=rows)[:, :, r0 % rows : r0 % rows + r1 - r0]
-            dst = woven_rows(b, r0, r1).bitcast(dtype).rearrange("p (r cc c2 u) -> p cc r c2 u", c2=2, u=2, r=r1 - r0)
+            src = src.rearrange("p u (c r) -> p u c r", r=rows)[:, :, :, r0 % rows : r0 % rows + r1 - r0]
+            run = min(r1 - r0, 4)
+            src = src.rearrange("p u c (q r) -> p q c u r", r=run)
+            dst = woven_rows(b, r0, r1).bitcast(dtype).rearrange("p (q r c u) -> p q c u r", r=run, c=COLS, u=2)
             return dst, src
 
         def weave_vector(b, r0, r1):
@@ -158,8 +165,8 @@ def tile_picked_listconv_relu_e_kernel(tc, xT, w1, w2, w3, offs, out):
                 res = woven_rows(2, 4, 6).bitcast(F32)
             else:
                 res = keep.tile([P, rows * COLS], F32, name=f"res_{b}_{m}")[:]
-            dst = res.rearrange("p (c r) -> p c r", r=rows)
-            src = acc[b][m][:].rearrange("p (r c) -> p c r", r=rows)
+            dst = res.rearrange("p (cc e r) -> p cc r e", e=2, r=rows)
+            src = acc[b][m][:].rearrange("p (r cc e) -> p cc r e", e=2, r=rows)
             if on_vector:
                 nc.vector.tensor_scalar_max(dst, src, 0.0)
             else:

@@ -43,11 +43,10 @@ def tile_picked_listconv_relu_e_kernel(tc, xT, w1, w2, w3, offs, out):
             nc.sync.dma_start(out=raw[:], in_=x_rows[:, 2 * u : 2 * u + 2, t0:t1])
             return raw
 
-        raw_a0 = load_x(0, 0, 1024)
-        raw_a1 = load_x(0, 1024, 2048)
+        raw_a = load_x(0, 0, T)
         nc.sync.dma_start(offsets[:], offs)
-        raw_b0 = load_x(1, 0, 1024)
-        raw_b1 = load_x(1, 1024, 1536)
+        raw_b0 = load_x(1, 0, 768)
+        raw_b1 = load_x(1, 768, 1536)
         raw_b2 = load_x(1, 1536, 2048)
         w_raw = {}
         for d in (2, 1, 0):
@@ -75,22 +74,20 @@ def tile_picked_listconv_relu_e_kernel(tc, xT, w1, w2, w3, offs, out):
         both = [t[:].rearrange("p (u g) -> p u g", u=2) for t in picked]
         nc.vector.memset(both[0][:, :, LEAD : LEAD + HALO], 0)
 
-        def gather(u, h):
-            first = max(h * HALF - LEAD, 0)
-            last = (h + 1) * HALF
+        def gather(u, h, first, last):
             at = first - (h * HALF - LEAD) + HALO
             nc.vector.tensor_copy(
                 both[h][:, u, at : at + last - first].bitcast(U32),
                 pairs[u][:].indirect(offsets[:, first // 16 : last // 16]),
             )
 
-        pair_vector(0, raw_a0, 0, 0, 1024)
-        pair_scalar(0, raw_a1, 1024, 1024, 1344)
-        pair_vector(0, raw_a1, 1024, 1344, 2048)
+        pair_scalar(0, raw_a, 0, 0, 704)
+        pair_vector(0, raw_a, 0, 704, T)
         for h in range(2):
-            gather(0, h)
-        pair_scalar(1, raw_b0, 0, 0, 1024)
-        pair_vector(1, raw_b1, 1024, 1024, 1536)
+            gather(0, h, max(h * HALF - LEAD, 0), (h + 1) * HALF)
+        pair_scalar(1, raw_b0, 0, 0, 768)
+        pair_scalar(1, raw_b1, 768, 768, 1280)
+        pair_vector(1, raw_b1, 768, 1280, 1536)
         pair_scalar(1, raw_b2, 1536, 1536, 1664)
         pair_vector(1, raw_b2, 1536, 1664, 2048)
 
@@ -119,8 +116,9 @@ def tile_picked_listconv_relu_e_kernel(tc, xT, w1, w2, w3, offs, out):
             dst = woven_rows(b, r0, r1).bitcast(dtype).rearrange("p (q r c u) -> p q c u r", r=run, c=COLS, u=2)
             return dst, src
 
-        def weave_vector(b, r0, r1):
-            nc.vector.tensor_copy(*weave_views(b, r0, r1, I32))
+        def weave_vector(b, r0, r1, c0, c1):
+            dst, src = weave_views(b, r0, r1, I32)
+            nc.vector.tensor_copy(dst[:, :, c0:c1], src[:, :, c0:c1])
 
         def weave_scalar(b, r0, r1):
             nc.scalar.copy(*weave_views(b, r0, r1, U32))
@@ -174,8 +172,10 @@ def tile_picked_listconv_relu_e_kernel(tc, xT, w1, w2, w3, offs, out):
             nc.sync.dma_start(out=out[m * P : (m + 1) * P, BLOCK_START[b] : BLOCK_START[b] + rows * COLS], in_=res)
 
         cast_w(2)
-        gather(1, 0)
-        weave_vector(0, 0, 8)
+        gather(1, 0, 0, 256)
+        gather(1, 0, 256, 512)
+        weave_vector(0, 0, 8, 0, 32)
+        weave_vector(0, 0, 8, 32, 64)
         weave_scalar(0, 8, 10)
         cast_w(1)
         cast_w(0)
@@ -183,14 +183,14 @@ def tile_picked_listconv_relu_e_kernel(tc, xT, w1, w2, w3, offs, out):
         quantize_x(0, 0, 8)
         quantize_w(1)
         quantize_x(0, 8, 10)
-        gather(1, 1)
+        gather(1, 1, HALF - LEAD, S)
         quantize_w(0)
         for d in (2, 1, 0):
             for m in range(2):
                 product(0, m, d)
-        weave_vector(1, 0, 4)
+        weave_vector(1, 0, 4, 0, COLS)
         weave_scalar(1, 4, 6)
-        weave_vector(2, 0, 4)
+        weave_vector(2, 0, 4, 0, COLS)
         weave_scalar(2, 4, 6)
         for b in range(1, NB):
             quantize_x(b, 0, 4)

from contextlib import ExitStack

import concourse.mybir as mybir

K, T, S, N = 512, 2048, 1024, 256
TAPS = 3
FLOPS = 2 * TAPS * K * N * S

F32 = mybir.dt.float32
BF16 = mybir.dt.bfloat16
I32 = mybir.dt.int32
U32 = mybir.dt.uint32
U16 = mybir.dt.uint16
U8 = mybir.dt.uint8
FP8X4 = mybir.dt.float8_e4m3fn_x4
COPY = mybir.ActivationFunctionType.Copy
RELU = mybir.ActivationFunctionType.Relu

P = 128
COLS = 64
BLOCK_ROWS = (8, 4, 4)
BLOCK_START = (0, 512, 768)
NB = len(BLOCK_ROWS)
HALF = S // 2
HALO = TAPS - 1
LEAD = 32
GW = 576
ROW_WORDS = 2 * COLS


def tile_picked_listconv_relu_e_kernel(tc, xT, w1, w2, w3, offs, out):
    nc = tc.nc
    with ExitStack() as ctx:
        keep = ctx.enter_context(tc.tile_pool(name="keep", bufs=1))
        shared = ctx.enter_context(tc.tile_pool(name="shared", bufs=1))
        psum = ctx.enter_context(tc.psum_pool(name="psum", bufs=1))

        x_rows = xT.rearrange("(p j) t -> p j t", j=4)
        offsets = keep.tile([P, S // 16], U16, name="offsets")

        def load_x(u, t0, t1):
            raw = keep.tile([P, 2, t1 - t0], F32, name=f"x_raw_{u}_{t0}")
            nc.sync.dma_start(out=raw[:], in_=x_rows[:, 2 * u : 2 * u + 2, t0:t1])
            return raw

        raw_a = load_x(0, 0, T)
        nc.sync.dma_start(offsets[:], offs)
        raw_b0 = load_x(1, 0, 768)
        raw_b1 = load_x(1, 768, 1536)
        raw_b2 = load_x(1, 1536, 2048)
        w_raw = {}
        for d in (2, 1, 0):
            if d == 2:
                w_raw[d] = shared.tile([P, 4, N], F32, name="w_raw_2", align_bytes=64, offset=0)
            else:
                w_raw[d] = keep.tile([P, 4, N], F32, name=f"w_raw_{d}", tag=f"w_raw_{d}", align_bytes=64)
            nc.sync.dma_start(out=w_raw[d][:], in_=(w1, w2, w3)[d].rearrange("(p j) n -> p j n", j=4))

        pairs = [keep.tile([P, T], U32, name=f"pairs_{u}") for u in range(2)]

        def pair_views(u, raw, t_raw, t0, t1):
            dst = pairs[u][:, t0:t1].bitcast(BF16).rearrange("p (t e) -> p t e", e=2)
            src = raw[:, :, t0 - t_raw : t1 - t_raw].rearrange("p e t -> p t e")
            return dst, src

        def pair_vector(u, raw, t_raw, t0, t1):
            nc.vector.tensor_copy(*pair_views(u, raw, t_raw, t0, t1))

        def pair_scalar(u, raw, t_raw, t0, t1):
            dst, src = pair_views(u, raw, t_raw, t0, t1)
            nc.scalar.activation(dst, src, COPY)

        picked = [keep.tile([P, 2 * GW], I32, name=f"picked_{h}", align_bytes=64) for h in range(2)]
        both = [t[:].rearrange("p (u g) -> p u g", u=2) for t in picked]
        nc.vector.memset(both[0][:, :, LEAD : LEAD + HALO], 0)

        def gather(u, h, first, last):
            at = first - (h * HALF - LEAD) + HALO
            nc.vector.tensor_copy(
                both[h][:, u, at : at + last - first].bitcast(U32),
                pairs[u][:].indirect(offsets[:, first // 16 : last // 16]),
            )

        pair_scalar(0, raw_a, 0, 0, 704)
        pair_vector(0, raw_a, 0, 704, T)
        for h in range(2):
            gather(0, h, max(h * HALF - LEAD, 0), (h + 1) * HALF)
        pair_scalar(1, raw_b0, 0, 0, 768)
        pair_scalar(1, raw_b1, 768, 768, 1280)
        pair_vector(1, raw_b1, 768, 1280, 1536)
        pair_scalar(1, raw_b2, 1536, 1536, 1664)
        pair_vector(1, raw_b2, 1536, 1664, 2048)

        w_bf_2 = keep.tile([P, N * 4], BF16, name="w_bf_2", align_bytes=64)
        w_bf_0 = keep.tile([P, N * 4], BF16, name="w_bf_0", align_bytes=64)
        w_bf = [w_bf_0[:], picked[1][:, GW : GW + 2 * N].bitcast(BF16), w_bf_2[:]]
        woven_0 = keep.tile([P, 8 * ROW_WORDS], I32, name="woven_0", align_bytes=64)
        halo_0 = shared.tile([P, HALO * ROW_WORDS], I32, name="halo_0", align_bytes=64, offset=0)
        woven_12 = keep.tile([P, 12 * ROW_WORDS], I32, name="woven_12", tag="w_raw_0", align_bytes=64)
        x_codes = [shared.tile([P, 10 * COLS], U32, name="x_codes_0", align_bytes=64, offset=1024)]
        x_codes.extend(keep.tile([P, 6 * COLS], U32, name=f"x_codes_{b}", align_bytes=64) for b in range(1, NB))
        x_scales = [keep.tile([P, (r + HALO) * COLS], U8, name=f"x_scales_{b}", align_bytes=64) for b, r in enumerate(BLOCK_ROWS)]

        def woven_rows(b, r0, r1):
            if b == 0:
                return halo_0[:] if r0 == 8 else woven_0[:, r0 * ROW_WORDS : r1 * ROW_WORDS]
            return woven_12[:, (6 * (b - 1) + r0) * ROW_WORDS : (6 * (b - 1) + r1) * ROW_WORDS]

        def weave_views(b, r0, r1, dtype):
            rows = BLOCK_ROWS[b]
            base = LEAD + BLOCK_START[b] % HALF + (r0 // rows) * rows
            src = both[BLOCK_START[b] // HALF][:, :, base : base + rows * COLS].bitcast(dtype)
            src = src.rearrange("p u (c r) -> p u c r", r=rows)[:, :, :, r0 % rows : r0 % rows + r1 - r0]
            run = min(r1 - r0, 4)
            src = src.rearrange("p u c (q r) -> p q c u r", r=run)
            dst = woven_rows(b, r0, r1).bitcast(dtype).rearrange("p (q r c u) -> p q c u r", r=run, c=COLS, u=2)
            return dst, src

        def weave_vector(b, r0, r1, c0, c1):
            dst, src = weave_views(b, r0, r1, I32)
            nc.vector.tensor_copy(dst[:, :, c0:c1], src[:, :, c0:c1])

        def weave_scalar(b, r0, r1):
            nc.scalar.copy(*weave_views(b, r0, r1, U32))

        def quantize_x(b, r0, r1):
            nc.vector.quantize_mx(
                out=x_codes[b][:, r0 * COLS : r1 * COLS].bitcast(FP8X4),
                scales=x_scales[b][:, r0 * COLS : r1 * COLS],
                in_=woven_rows(b, r0, r1).bitcast(BF16),
            )

        w_codes = [keep.tile([P, N], U32, name=f"w_codes_{d}", align_bytes=64) for d in range(TAPS)]
        w_scales = [keep.tile([P, N], U8, name=f"w_scales_{d}", align_bytes=64) for d in range(TAPS)]

        def cast_w(d):
            nc.scalar.activation(
                w_bf[d].rearrange("p (c i j) -> p c j i", i=4, j=4),
                w_raw[d][:].rearrange("p j (c i) -> p c j i", i=4),
                COPY,
            )

        def quantize_w(d):
            nc.vector.quantize_mx(out=w_codes[d][:].bitcast(FP8X4), scales=w_scales[d][:], in_=w_bf[d])

        acc = [[psum.tile([P, r * COLS], F32, name=f"acc_{b}_{m}") for m in range(2)] for b, r in enumerate(BLOCK_ROWS)]

        def product(b, m, d):
            cols = slice((HALO - d) * COLS, (HALO - d + BLOCK_ROWS[b]) * COLS)
            nc.tensor.matmul_mx(
                out=acc[b][m][:],
                lhsT=w_codes[d][:, m * P : (m + 1) * P].bitcast(FP8X4),
                lhsT_scale=w_scales[d][:, m * P : (m + 1) * P],
                rhs=x_codes[b][:, cols].bitcast(FP8X4),
                rhs_scale=x_scales[b][:, cols],
                start=(d == TAPS - 1),
                stop=(d == 0),
            )

        def finish(b, m, on_vector):
            rows = BLOCK_ROWS[b]
            if (b, m) == (1, 0):
                res = woven_rows(2, 4, 6).bitcast(F32)
            else:
                res = keep.tile([P, rows * COLS], F32, name=f"res_{b}_{m}")[:]
            dst = res.rearrange("p (cc e r) -> p cc r e", e=2, r=rows)
            src = acc[b][m][:].rearrange("p (r cc e) -> p cc r e", e=2, r=rows)
            if on_vector:
                nc.vector.tensor_scalar_max(dst, src, 0.0)
            else:
                nc.scalar.activation(dst, src, RELU)
            nc.sync.dma_start(out=out[m * P : (m + 1) * P, BLOCK_START[b] : BLOCK_START[b] + rows * COLS], in_=res)

        cast_w(2)
        gather(1, 0, 0, 256)
        gather(1, 0, 256, 512)
        weave_vector(0, 0, 8, 0, 32)
        weave_vector(0, 0, 8, 32, 64)
        weave_scalar(0, 8, 10)
        cast_w(1)
        cast_w(0)
        quantize_w(2)
        quantize_x(0, 0, 8)
        quantize_w(1)
        quantize_x(0, 8, 10)
        gather(1, 1, HALF - LEAD, S)
        quantize_w(0)
        for d in (2, 1, 0):
            for m in range(2):
                product(0, m, d)
        weave_vector(1, 0, 4, 0, COLS)
        weave_scalar(1, 4, 6)
        weave_vector(2, 0, 4, 0, COLS)
        weave_scalar(2, 4, 6)
        for b in range(1, NB):
            quantize_x(b, 0, 4)
            quantize_x(b, 4, 6)
        finish(0, 0, False)
        finish(0, 1, False)
        for b in range(1, NB):
            for m in range(2):
                for d in (2, 1, 0):
                    product(b, m, d)
                finish(b, m, m == 0)
